import numpy as np, ml_dtypes
CORES = [3,11,19,27,35,43,51,59]
N = 8
import mx_ref
BF = ml_dtypes.bfloat16
def entries(a):
    return np.ascontiguousarray(a.T).reshape(-1)
def table(e):
    return np.ascontiguousarray(np.reshape(e, (-1, 16)).T).astype(np.int32)
def cols(t, e):
    v = np.concatenate([t.reshape(128, -1, 4), np.zeros((128, 1, 4), BF)], axis=1)
    return np.ascontiguousarray(v[:, e]).reshape(128, -1)
def f(rng, *shape):
    return mx_ref.flush((rng.standard_normal(shape, dtype=np.float32) * np.exp2(rng.integers(-2, 3, shape[:-1] + (1,)))).astype(BF))
def wide(rng, *shape, cols=0):
    v = rng.standard_normal(shape, dtype=np.float32) * np.exp2(rng.integers(-12, 13, shape)).astype(np.float32)
    if cols: v *= np.repeat(np.exp2(rng.integers(-cols, cols + 1, shape[:-2] + (1, shape[-1] // 4))) * (rng.random(shape[:-2] + (1, shape[-1] // 4)) > 0.0625), 4, axis=-1).astype(np.float32)
    return mx_ref.flush(v.astype(BF))
TA, TB, CI, CJ, JW = 256, 256, 24, 64, 384
SIDE = [r // 4 for r in range(N)]
GCOL = [SIDE[:r].count(SIDE[r]) for r in range(N)]
def fill(rng, total, cap, wd, first, back):
    n = np.zeros(N, int)
    for q in first: n[q] = min(cap, total - n.sum())
    while n.sum() < total:
        q = rng.integers(0, N)
        if n[q] < cap: n[q] += 1
    s, used = np.full((N, cap), -1), []
    for q in range(N):
        k, v = rng.permutation(cap)[:n[q]], rng.integers(0, wd, n[q])
        if back: k, v = np.sort(k), np.sort(v)[::-1]
        s[q, k] = v; used += list(q * cap + k)
    return s, (np.sort(used)[::-1] if back else rng.permutation(used))
def lists(rng, full=False, own=False, back=False, alike=False):
    A, B = [], []
    for i in range(2):
        A.append(fill(rng, 128, CI, TA, rng.permutation(N) if full else [r for r in range(N) if own and SIDE[r] == i], back))
    for k in range(4):
        B.append(fill(rng, JW, CJ, TB, rng.permutation(N) if full else [r for r in range(N) if own and GCOL[r] == k], back))
    if alike: B = [B[0]] * 4
    return {"sa": np.stack([table(np.concatenate([A[i][0][q] for i in range(2)])) for q in range(N)]),
            "sb": np.stack([table(np.concatenate([B[k][0][q] for k in range(4)])) for q in range(N)]),
            "pi": np.stack([table(A[SIDE[r]][1]) for r in range(N)]), "pj": np.stack([table(B[GCOL[r]][1]) for r in range(N)])}
def setup_inputs(rng):
    return {"a": f(rng, N, 128, 4 * TA), "b": f(rng, N, 128, 4 * TB), **lists(rng)}
def setup_inputs_alike(rng):
    return {**setup_inputs(rng), **lists(rng, alike=True)}
def setup_inputs_full(rng):
    return {**setup_inputs(rng), **lists(rng, full=True)}
def setup_inputs_own(rng):
    return {**setup_inputs(rng), **lists(rng, own=True)}
def setup_inputs_reversed(rng):
    return {**setup_inputs(rng), **lists(rng, back=True)}
def setup_inputs_spread(rng):
    d = setup_inputs(rng); d["a"], d["b"] = wide(rng, N, 128, 4 * TA, cols=6), wide(rng, N, 128, 4 * TB, cols=6); return d
def check_inputs(d):
    bad = []
    for s, p, wd, cap, total, place in (("sa", "pi", TA, CI, 128, SIDE), ("sb", "pj", TB, CJ, JW, GCOL)):
        e = np.stack([entries(d[s][q]) for q in range(N)])
        if e.min() < -1 or e.max() >= wd: bad.append(s)
        for r in range(N):
            v = e[:, cap * place[r]:cap * place[r] + cap].reshape(-1)
            if (v >= 0).sum() != total: bad.append(s + " count")
            t = entries(d[p][r])
            if t.min() < 0 or t.max() >= N * cap: bad.append(p); continue
            if len(set(t.tolist())) != total or (v[t] < 0).any(): bad.append(p + " slots")
            if (d[p][r] != d[p][place.index(place[r])]).any(): bad.append(p + " not the same")
    return bad
def reference(a, b, sa, sb, pi, pj):
    y = np.zeros((N, 128, JW), np.float32)
    for r in range(N):
        i, k = SIDE[r], GCOL[r]
        A = np.concatenate([cols(a[q], entries(sa[q])[CI * i:CI * i + CI]) for q in range(N)], axis=1)
        B = np.concatenate([cols(b[q], entries(sb[q])[CJ * k:CJ * k + CJ]) for q in range(N)], axis=1)
        y[r] = mx_ref.matmul(mx_ref.quantize(cols(A, entries(pi[r]))), mx_ref.quantize(cols(B, entries(pj[r]))))
    return {"y": y}

@@ -1,0 +1,351 @@
+from concourse.bass import DstId, RemoteDMATransfer, IndirectOffsetOnAxis
+from concourse.mybir import dt, AluOpType, AxisListType, ActivationFunctionType
+
+CORES = [3, 11, 19, 27, 35, 43, 51, 59]
+N = 8
+TA, TB, CI, CJ, JW, M = 256, 256, 24, 64, 384, 128
+SIDE = [r // 4 for r in range(N)]
+GCOL = [r % 4 for r in range(N)]
+W = 2 * CI + 4 * CJ
+PAIR = 2 * CJ
+FARW = PAIR + 2 * CI
+NEARW = PAIR + CI
+APOS = PAIR
+LA0 = 8
+SA, SB = N * CI, N * CJ
+KB, KA = 16, 3
+LST = KB + KA
+UW = 20
+
+SCRATCH = {
+    "wa": ("sbuf", [128, 4 * TA], "bfloat16"),
+    "wb": ("sbuf", [128, 4 * TB], "bfloat16"),
+    "lst": ("sbuf", [128, LST], "int32"),
+    "off": ("sbuf", [128, 4 * UW], "uint16"),
+    "h": ("sbuf", [128, 4 * W], "bfloat16"),
+    "qc": ("sbuf", [128, W], "float8_e4m3fn_x4"),
+    "qs": ("sbuf", [128, W], "uint8"),
+    "hfc": ("sbuf", [128, FARW], "float8_e4m3fn_x4"),
+    "hnc": ("sbuf", [128, NEARW], "float8_e4m3fn_x4"),
+    "hs": ("sbuf", [128, W], "uint8"),
+    "lac": ("sbuf", [128, 304], "float8_e4m3fn_x4"),
+    "las": ("sbuf", [128, 304], "uint8"),
+    "lbc": ("sbuf", [128, SB + CJ], "float8_e4m3fn_x4"),
+    "lbs": ("sbuf", [128, SB + CJ], "uint8"),
+    "pil": ("sbuf", [128, 8], "int32"),
+    "pit": ("sbuf", [128, 8], "int32"),
+    "pim": ("sbuf", [128, 8], "int32"),
+    "pio": ("sbuf", [128, 8], "uint16"),
+    "pjl": ("sbuf", [128, 24], "int32"),
+    "pjt": ("sbuf", [128, 24], "int32"),
+    "pju": ("sbuf", [128, 24], "int32"),
+    "pjo": ("sbuf", [128, 24], "uint16"),
+    "part": ("sbuf", [128, 1], "int32"),
+    "part16": ("sbuf", [128, 1], "int32"),
+    "count": ("sbuf", [128, 128], "float32"),
+    "ones": ("sbuf", [128, 128], "float32"),
+    "eye": ("sbuf", [128, 128], "float32"),
+    "inv": ("sbuf", [128, SA], "float32"),
+    "dg1": ("sbuf", [128, 128], "float32"),
+    "dg2": ("sbuf", [128, 128], "float32"),
+    "ix1f": ("sbuf", [128, 1], "float32"),
+    "ix2f": ("sbuf", [128, 1], "float32"),
+    "ix1": ("sbuf", [128, 1], "int32"),
+    "ix2": ("sbuf", [128, 1], "int32"),
+    "s1": ("sbuf", [128, SB], "float32"),
+    "s2": ("sbuf", [128, SB], "float32"),
+    "y1": ("sbuf", [128, JW], "float32"),
+    "y2": ("sbuf", [128, JW], "float32"),
+    "ps": ("psum", [128, 4 * 512], "float32"),
+}
+SEMAPHORES = ["lists", "ldb", "lda", "ldpi", "ldpj", "iota", "cnt", "eyed", "onesd", "filled", "p16", "offs", "offv",
+              "fars", "farv", "nears", "nearv", "qfar", "qnear", "qown", "vc", "ixd",
+              "hopf", "hopn", "hops", "arr", "sent",
+              "m0", "m1", "m2", "m3", "c1v", "c1s", "c2v", "c2s", "yd1", "yd2", "ystored"]
+
+
+def layout(q):
+    if SIDE[q] == 1:
+        return 0, APOS + 2 * CI, APOS, 0
+    return APOS + 2 * CI, 0, 0, APOS + CI
+
+
+def bcol(q, d):
+    near, far, _, _ = layout(q)
+    return (near if GCOL[d] // 2 == GCOL[q] // 2 else far) + CJ * (GCOL[d] % 2)
+
+
+def acol(d):
+    return APOS + CI * SIDE[d]
+
+
+def bland(d, q):
+    if GCOL[d] % 2 == 0:
+        return 0, (q - d - 1) % N
+    return CJ, (q - d) % N
+
+
+def aland(d, q):
+    return LA0 + CI * ((q - d - 1) % N)
+
+
+def plan(topo, q):
+    me = CORES[q]
+    mate = [d for d in range(N) if topo.mates(topo.chip(me), topo.chip(CORES[d]))][0]
+    near = lambda d: GCOL[d] // 2 == GCOL[q] // 2
+    same = [d for d in range(N) if d != q and topo.same_plane(topo.chip(me), topo.chip(CORES[d]))]
+    cross = [d for d in range(N) if d != q and d != mate and d not in same]
+    sn, sf = [d for d in same if near(d)], [d for d in same if not near(d)]
+    xn, xf = [d for d in cross if near(d)], [d for d in cross if not near(d)]
+    others = [c for c in topo.cores_of(me) if c != me]
+    ported = [c for c in others if topo.may_write(c, CORES[mate])]
+    plain = [c for c in others if c not in ported]
+    here = lambda c: topo.die(c) == topo.die(me)
+    c_xn = [c for c in ported if here(c)][0]
+    c_xfc, c_xfs = [c for c in ported if not here(c)][:2]
+    c_sfc, c_sfs = [c for c in plain if here(c)][:2]
+    c_snc, c_sns = [c for c in plain if not here(c)][:2]
+    hops = {"far": [c_xfc, c_sfc], "scales": [c_xfs, c_sfs, c_sns], "near": [c_xn, c_snc]}
+    sends = [(me, "codes", [mate], "tile"), (me, "scales", [mate] + xn, "tile"),
+             (c_xn, "codes", xn, "near"), (c_snc, "codes", sn, "near"),
+             (c_xfc, "codes", xf, "far"), (c_sfc, "codes", sf, "far"),
+             (c_xfs, "scales", xf, "scales"), (c_sfs, "scales", sf, "scales"), (c_sns, "scales", sn, "scales")]
+    return hops, sends
+
+
+def engine_parts(topo, src, dsts):
+    e = topo.engines(src, CORES[dsts[0]])
+    k = len(e) // len(dsts)
+    return [sum(1 << x for x in e[i * k:(i + 1) * k]) for i in range(len(dsts))]
+
+
+def dst_id(topo, c):
+    rid, pid, _ = topo.addr(c)
+    return DstId(rid=rid, pnc=pid)
+
+
+def hop(g, T, topo, core, src, dst, helpers, sem):
+    g.remote_dma_fused([RemoteDMATransfer(dst_ids=[dst_id(topo, c) for c in helpers],
+                                          dma_engine_mask=topo.mask(core, helpers[0]), remote_sem=T.sem[sem],
+                                          srcs=[src], dsts=[dst for _ in helpers], alu_op=0)], local_sem=T.sem.sent)
+    return len(topo.engines(core, helpers[0]))
+
+
+def send(g, T, topo, core, q, kind, dsts, source):
+    _, _, farb, nearb = layout(q)
+    buf, base = {"tile": ("qc" if kind == "codes" else "qs", 0), "far": ("hfc", farb), "near": ("hnc", nearb),
+                 "scales": ("hs", 0)}[source]
+    used = 0
+    for tile in ("b", "a"):
+        tr = []
+        for d, m in zip(dsts, engine_parts(topo, core, dsts)):
+            if tile == "b":
+                view, pos = bland(d, q)
+                s, e, w, land = bcol(q, d) - base, view + CJ * pos, CJ, "lb"
+            else:
+                s, e, w, land = acol(d) - base, aland(d, q), CI, "la"
+            if kind == "codes":
+                src, dst = T[buf][:, s:s + w].bitcast(dt.uint8), T[land + "c"][:, e:e + w].bitcast(dt.uint8)
+            else:
+                src, dst = T[buf][:, s:s + w], T[land + "s"][:, e:e + w]
+            tr.append(RemoteDMATransfer(dst_ids=[dst_id(topo, CORES[d])], dma_engine_mask=m, remote_sem=T.sem.arr,
+                                        srcs=[src], dsts=[dst], alu_op=0))
+            used += bin(m).count("1")
+        g.remote_dma_fused(tr, local_sem=T.sem.sent)
+    return used
+
+
+def arrivals(topo, r):
+    n = 0
+    for q in range(N):
+        if q != r:
+            for c, _, dsts, _ in plan(topo, q)[1]:
+                for d, m in zip(dsts, engine_parts(topo, c, dsts)):
+                    n += 2 * bin(m).count("1") if d == r else 0
+    return n
+
+
+def helper_program(g, core, T, topo, q):
+    hops, sends = plan(topo, q)
+    sem = {"far": "hopf", "near": "hopn", "scales": "hops"}
+    used = 0
+    for c, kind, dsts, source in sends:
+        if c == core:
+            g.wait_ge(T.sem[sem[source]], len(topo.engines(CORES[q], core)))
+            used += send(g, T, topo, core, q, kind, dsts, source)
+    if used:
+        g.wait_ge(T.sem.sent, used)
+
+
+def rank_program(g, core, T, topo):
+    rank = T.rank_of(core)
+    if rank is None:
+        q = [r for r in range(N) if topo.chip(CORES[r]) == topo.chip(core)]
+        if q:
+            helper_program(g, core, T, topo, q[0])
+        return
+    v, sc, sy, te, sem = g.vector, g.scalar, g.sync, g.tensor, T.sem
+    COPY = ActivationFunctionType.Copy
+    hops, sends = plan(topo, rank)
+    near, far, farb, nearb = layout(rank)
+    kn = 8 * (GCOL[rank] // 2)
+    kf = 8 - kn
+    oa = acol(rank)
+
+    sy.dma_start(T.wb[:], T.b[:]).then_inc(sem.ldb, 16)
+    for k in range(8):
+        sy.dma_start(T.lst[16 * k:16 * k + 16, 0:KB], T.sb[:]).then_inc(sem.lists, 16)
+        sc.dma_start(T.lst[16 * k:16 * k + 16, KB:LST], T.sa[:]).then_inc(sem.lists, 16)
+    sc.dma_start(T.wa[:], T.a[:]).then_inc(sem.lda, 16)
+    for k in range(8):
+        sy.dma_start(T.pil[16 * k:16 * k + 16, :], T.pi[:]).then_inc(sem.ldpi, 16)
+
+    g.iota(T.part[:], [[1, 1]], 0, 1).then_inc(sem.iota, 1)
+    g.iota(T.count[:], [[1, 128]], 0, 0, allow_small_or_imprecise_dtypes=True).then_inc(sem.cnt, 1)
+    g.wait_ge(sem.p16, 1)
+    g.indirect_dma_start(out=T.pjl[:, 0:24], out_offset=None, in_=T.pj[:],
+                         in_offset=IndirectOffsetOnAxis(ap=T.part16[:, 0:1], axis=0),
+                         bounds_check=15).then_inc(sem.ldpj, 16)
+    g.wait_ge(sem.onesd, 1)
+    g.affine_select(T.eye[:], T.ones[:], [[-1, 128]], AluOpType.is_equal, 0.0, 0, 1).then_inc(sem.eyed, 1)
+
+    used = 0
+    g.wait_ge(sem.qfar, 1)
+    used += hop(g, T, topo, core, T.qc[:, farb:farb + FARW].bitcast(dt.uint8), T.hfc[:, 0:FARW].bitcast(dt.uint8),
+                hops["far"], "hopf")
+    g.wait_ge(sem.qnear, 1)
+    used += hop(g, T, topo, core, T.qs[:, 0:W], T.hs[:, 0:W], hops["scales"], "hops")
+    used += hop(g, T, topo, core, T.qc[:, nearb:nearb + NEARW].bitcast(dt.uint8), T.hnc[:, 0:NEARW].bitcast(dt.uint8),
+                hops["near"], "hopn")
+    for c, kind, dsts, source in sends:
+        if c == core:
+            used += send(g, T, topo, core, rank, kind, dsts, source)
+
+    v.memset(T.ones[:], 1.0).then_inc(sem.onesd, 1)
+    v.memset(T.inv[:], 999.0).then_inc(sem.filled, 1)
+    v.wait_ge(sem.iota, 1)
+    v.tensor_scalar(T.part16[:], T.part[:], 15, None, AluOpType.bitwise_and).then_inc(sem.p16, 1)
+
+    def offsets(t, s):
+        v.tensor_scalar(T.off[:, UW * t:UW * t + LST], T.lst[:], 4, t, AluOpType.mult, AluOpType.add).then_inc(sem[s], 1)
+
+    def blocks(t, what):
+        if what == "a":
+            return T.h[:, 4 * APOS + t:4 * (APOS + 2 * CI):4], T.wa[:].indirect(T.off[:, UW * t + KB:UW * t + LST])
+        k, p = (kn, near) if what == "near" else (kf, far)
+        return T.h[:, 4 * p + t:4 * (p + PAIR):4], T.wb[:].indirect(T.off[:, UW * t + k:UW * t + k + 8])
+
+    def gather_v(t, what, s):
+        o, i = blocks(t, what)
+        v.tensor_copy(o, i).then_inc(sem[s], 1)
+
+    def gather_s(t, what, s):
+        o, i = blocks(t, what)
+        sc.activation(o, i, COPY).then_inc(sem[s], 1)
+
+    v.wait_ge(sem.lists, 256)
+    for t in (2, 3):
+        offsets(t, "offs")
+    for t in (0, 1):
+        offsets(t, "offv")
+    sc.wait_ge(sem.offs, 2)
+    sc.wait_ge(sem.ldb, 16)
+    v.wait_ge(sem.offv, 2)
+    v.wait_ge(sem.ldb, 16)
+    gather_s(2, "far", "fars")
+    gather_s(3, "far", "fars")
+    sc.wait_ge(sem.offv, 2)
+    sc.wait_ge(sem.lda, 16)
+    for t in (1, 2, 3):
+        gather_s(t, "a", "fars")
+    gather_v(0, "far", "farv")
+    gather_v(1, "far", "farv")
+    v.wait_ge(sem.lda, 16)
+    gather_v(0, "a", "farv")
+    gather_s(2, "near", "nears")
+    gather_s(3, "near", "nears")
+    v.wait_ge(sem.farv, 3)
+    v.wait_ge(sem.fars, 5)
+    v.quantize_mx(T.qc[:, farb:farb + FARW], T.qs[:, farb:farb + FARW],
+                  T.h[:, 4 * farb:4 * (farb + FARW)]).then_inc(sem.qfar, 1)
+    gather_v(0, "near", "nearv")
+    gather_v(1, "near", "nearv")
+    v.wait_ge(sem.nearv, 2)
+    v.wait_ge(sem.nears, 2)
+    v.quantize_mx(T.qc[:, near:near + PAIR], T.qs[:, near:near + PAIR],
+                  T.h[:, 4 * near:4 * (near + PAIR)]).then_inc(sem.qnear, 1)
+    view, pos = bland(rank, rank)
+    e = view + CJ * pos - CJ * (GCOL[rank] % 2)
+    v.quantize_mx(T.lbc[:, e:e + PAIR], T.lbs[:, e:e + PAIR], T.h[:, 4 * near:4 * (near + PAIR)]).then_inc(sem.qown, 1)
+    e = aland(rank, rank)
+    v.quantize_mx(T.lac[:, e:e + 128], T.las[:, e:e + 128], T.h[:, 4 * oa:4 * (oa + 128)]).then_inc(sem.qown, 1)
+
+    n = [0]
+
+    def done(ins):
+        ins.then_inc(sem.vc, 1)
+        n[0] += 1
+
+    def settle():
+        v.wait_ge(sem.vc, n[0])
+    pos0 = bland(rank, 0)[1]
+    ca = aland(rank, 0) - LA0
+    A = AluOpType
+    v.wait_ge(sem.ldpi, 128)
+    done(v.tensor_scalar(T.pit[:], T.pil[:], ca, None, A.add))
+    v.wait_ge(sem.ldpj, 16)
+    done(v.tensor_scalar(T.pjt[:], T.pjl[:], CJ * pos0, None, A.add))
+    settle()
+    done(v.tensor_scalar(T.pim[:], T.pit[:], SA, -SA, A.is_ge, A.mult))
+    done(v.tensor_scalar(T.pju[:], T.pjt[:], SB - 1, None, A.bitwise_and))
+    settle()
+    done(v.tensor_tensor(T.pit[:], T.pit[:], T.pim[:], A.add))
+    done(v.tensor_copy(T.pjo[:], T.pju[:]))
+    settle()
+    done(v.tensor_copy(T.pio[:], T.pit[:]))
+    settle()
+    v.wait_ge(sem.filled, 1)
+    v.wait_ge(sem.cnt, 1)
+    done(v.tensor_copy(T.inv[:].indirect(T.pio[:, 0:8]), T.count[:]))
+    settle()
+    v.wait_ge(sem.eyed, 1)
+    done(v.tensor_tensor(T.dg1[:], T.inv[:, CJ:SA], T.eye[:], A.mult))
+    done(v.tensor_tensor(T.dg2[:], T.inv[:, 0:128], T.eye[:], A.mult))
+    settle()
+    done(v.tensor_reduce(T.ix1f[:], T.dg1[:], AxisListType.X, A.add))
+    done(v.tensor_reduce(T.ix2f[:], T.dg2[:], AxisListType.X, A.add))
+    settle()
+    v.tensor_copy(T.ix1[:], T.ix1f[:]).then_inc(sem.ixd, 1)
+    v.tensor_copy(T.ix2[:], T.ix2f[:]).then_inc(sem.ixd, 1)
+    sc.wait_ge(sem.vc, n[0])
+
+    te.wait_ge(sem.qown, 2)
+    te.wait_ge(sem.arr, arrivals(topo, rank))
+    hb = SB // 2
+    for i in range(4):
+        a0, b0 = LA0 + (SA - 128 if i < 2 else 0), view + hb * (i % 2)
+        te.matmul_mx(T.ps[:, 512 * i:512 * i + hb], T.lac[:, a0:a0 + 128], T.las[:, a0:a0 + 128],
+                     T.lbc[:, b0:b0 + hb], T.lbs[:, b0:b0 + hb], True, True).then_inc(sem["m%d" % i], 1)
+    for i in (1, 2):
+        s, y, hy = T["s%d" % i], T["y%d" % i], JW // 2
+        cv, cs, yd = sem["c%dv" % i], sem["c%ds" % i], sem["yd%d" % i]
+        p = 1024 * (i - 1)
+        v.wait_ge(sem["m%d" % (2 * i - 2)], 1)
+        v.tensor_copy(s[:, 0:hb], T.ps[:, p:p + hb]).then_inc(cv, 1)
+        sc.wait_ge(sem["m%d" % (2 * i - 1)], 1)
+        sc.activation(s[:, hb:SB], T.ps[:, p + 512:p + 512 + hb], COPY).then_inc(cs, 1)
+        v.wait_ge(cv, 1)
+        v.wait_ge(cs, 1)
+        v.tensor_copy(y[:, 0:hy], s[:].indirect(T.pjo[:, 0:12])).then_inc(yd, 1)
+        sc.wait_ge(cv, 1)
+        sc.wait_ge(cs, 1)
+        sc.activation(y[:, hy:JW], s[:].indirect(T.pjo[:, 12:24]), COPY).then_inc(yd, 1)
+
+    g.wait_ge(sem.ixd, 2)
+    for i, rows in ((1, 128), (2, SA - 128)):
+        g.wait_ge(sem["yd%d" % i], 2)
+        g.indirect_dma_start(out=T.y[:], out_offset=IndirectOffsetOnAxis(ap=T["ix%d" % i][0:rows, 0:1], axis=0),
+                             in_=T["y%d" % i][0:rows, 0:JW], in_offset=None, bounds_check=M - 1,
+                             oob_is_err=False).then_inc(sem.ystored, 16)
+    g.wait_ge(sem.sent, used)
+    g.wait_ge(sem.ystored, 32)

@@ -6,35 +6,38 @@ N = 8
 TA, TB, CI, CJ, JW, M = 256, 256, 24, 64, 384, 128
 SIDE = [r // 4 for r in range(N)]
 GCOL = [r % 4 for r in range(N)]
-W = 2 * CI + 4 * CJ
 PAIR = 2 * CJ
-FARW = PAIR + 2 * CI
-NEARW = PAIR + CI
-APOS = PAIR
-LA0 = 8
 SA, SB = N * CI, N * CJ
 KB, KA = 16, 3
-LST = KB + KA
-UW = 20
+LAW = 304
+ZA = 128 - 2 * CI
+CHUNKS = ((0, 3 * CJ), (3 * CJ, 5 * CJ), (5 * CJ, 8 * CJ))
 
 SCRATCH = {
     "wa": ("sbuf", [128, 4 * TA], "bfloat16"),
     "wb": ("sbuf", [128, 4 * TB], "bfloat16"),
-    "lst": ("sbuf", [128, LST], "int32"),
-    "off": ("sbuf", [128, 4 * UW], "uint16"),
-    "h": ("sbuf", [128, 4 * W], "bfloat16"),
-    "qc": ("sbuf", [128, W], "float8_e4m3fn_x4"),
-    "qs": ("sbuf", [128, W], "uint8"),
-    "hfc": ("sbuf", [128, FARW], "float8_e4m3fn_x4"),
-    "hnc": ("sbuf", [128, NEARW], "float8_e4m3fn_x4"),
-    "hs": ("sbuf", [128, W], "uint8"),
-    "lac": ("sbuf", [128, 304], "float8_e4m3fn_x4"),
-    "las": ("sbuf", [128, 304], "uint8"),
+    "lsb": ("sbuf", [128, KB], "int32"),
+    "lsa": ("sbuf", [128, KA], "int32"),
+    "offb": ("sbuf", [128, 4 * KB], "uint16"),
+    "offa": ("sbuf", [128, 16], "uint16"),
+    "tf": ("sbuf", [128, 4 * PAIR], "bfloat16"),
+    "tn": ("sbuf", [128, 4 * PAIR], "bfloat16"),
+    "ta": ("sbuf", [128, 4 * 128], "bfloat16"),
+    "qc": ("sbuf", [128, PAIR], "float8_e4m3fn_x4"),
+    "qs": ("sbuf", [128, PAIR], "uint8"),
+    "hfc": ("sbuf", [128, CJ], "float8_e4m3fn_x4"),
+    "hfs": ("sbuf", [128, CJ], "uint8"),
+    "hnc": ("sbuf", [128, CJ], "float8_e4m3fn_x4"),
+    "hns": ("sbuf", [128, CJ], "uint8"),
+    "hac": ("sbuf", [128, 2 * CI], "float8_e4m3fn_x4"),
+    "has": ("sbuf", [128, 2 * CI], "uint8"),
+    "lac": ("sbuf", [128, LAW], "float8_e4m3fn_x4"),
+    "las": ("sbuf", [128, LAW], "uint8"),
     "lbc": ("sbuf", [128, SB + CJ], "float8_e4m3fn_x4"),
     "lbs": ("sbuf", [128, SB + CJ], "uint8"),
     "pil": ("sbuf", [128, 8], "int32"),
     "pit": ("sbuf", [128, 8], "int32"),
-    "pim": ("sbuf", [128, 8], "int32"),
+    "pim": ("sbuf", [128, 8 * N], "int32"),
     "pio": ("sbuf", [128, 8], "uint16"),
     "pjl": ("sbuf", [128, 24], "int32"),
     "pjt": ("sbuf", [128, 24], "int32"),
@@ -42,10 +45,10 @@ SCRATCH = {
     "pjo": ("sbuf", [128, 24], "uint16"),
     "part": ("sbuf", [128, 1], "int32"),
     "part16": ("sbuf", [128, 1], "int32"),
+    "partf": ("sbuf", [128, 1], "float32"),
     "count": ("sbuf", [128, 128], "float32"),
-    "ones": ("sbuf", [128, 128], "float32"),
     "eye": ("sbuf", [128, 128], "float32"),
-    "inv": ("sbuf", [128, SA], "float32"),
+    "inv": ("sbuf", [128, LAW], "float32"),
     "dg1": ("sbuf", [128, 128], "float32"),
     "dg2": ("sbuf", [128, 128], "float32"),
     "ix1f": ("sbuf", [128, 1], "float32"),
@@ -56,27 +59,12 @@ SCRATCH = {
     "s2": ("sbuf", [128, SB], "float32"),
     "y1": ("sbuf", [128, JW], "float32"),
     "y2": ("sbuf", [128, JW], "float32"),
-    "ps": ("psum", [128, 4 * 512], "float32"),
+    "ps": ("psum", [128, 6 * 512], "float32"),
 }
-SEMAPHORES = ["lists", "ldb", "lda", "ldpi", "ldpj", "iota", "cnt", "eyed", "onesd", "filled", "p16", "offs", "offv",
-              "fars", "farv", "nears", "nearv", "qfar", "qnear", "qown", "vc", "ixd",
-              "hopf", "hopn", "hops", "arr", "sent",
-              "m0", "m1", "m2", "m3", "c1v", "c1s", "c2v", "c2s", "yd1", "yd2", "ystored"]
-
-
-def layout(q):
-    if SIDE[q] == 1:
-        return 0, APOS + 2 * CI, APOS, 0
-    return APOS + 2 * CI, 0, 0, APOS + CI
-
-
-def bcol(q, d):
-    near, far, _, _ = layout(q)
-    return (near if GCOL[d] // 2 == GCOL[q] // 2 else far) + CJ * (GCOL[d] % 2)
-
-
-def acol(d):
-    return APOS + CI * SIDE[d]
+SEMAPHORES = ["listb", "lista", "ldb", "lda", "ldpi", "ldpj", "iota", "cnt", "filled", "zeros", "p16", "pf",
+              "off2", "off3", "offv", "offa", "fars", "farv", "nears", "nearv", "as", "av", "qf", "qn", "qa", "vc", "ixd",
+              "hfc", "hfs", "hnc", "hns", "hac", "has", "arre", "arrl", "arr0", "arr1", "arr2", "arr3", "sent",
+              "m0", "m1", "m2", "m3", "m4", "m5", "c1v", "c1s", "c2v", "c2s", "yd1", "yd2", "ystored"]
 
 
 def bland(d, q):
@@ -85,94 +73,137 @@ def bland(d, q):
     return CJ, (q - d) % N
 
 
-def aland(d, q):
-    return LA0 + CI * ((q - d - 1) % N)
+def near_at(r):
+    view, pos = bland(r, r)
+    return view + CJ * pos - CJ * (GCOL[r] % 2)
+
+
+def bsrc(q, d):
+    if GCOL[d] // 2 == GCOL[q] // 2:
+        return "lbc", "lbs", near_at(q) + CJ * (GCOL[d] % 2)
+    return "qc", "qs", CJ * (GCOL[d] % 2)
+
+
+def a_run(r):
+    return (176, 176) if SIDE[r] == 0 else (0, ZA)
+
+
+def away(d, q):
+    return (q // 2 - d // 2) % 4
+
+
+def groups(topo, q):
+    chip = [topo.chip(c) for c in CORES]
+    mate = [d for d in range(N) if topo.mates(chip[q], chip[d])][0]
+    same = [d for d in range(N) if d != q and topo.same_plane(chip[q], chip[d])]
+    cross = [d for d in range(N) if d not in same + [q, mate]]
+    near = lambda ds: [d for d in ds if GCOL[d] // 2 == GCOL[q] // 2]
+    far = lambda ds: [d for d in ds if GCOL[d] // 2 != GCOL[q] // 2]
+    return mate, near(same), far(same), near(cross), far(cross)
+
+
+def aland(topo, d):
+    mate, _, _, xn, _ = groups(topo, d)
+    late = [q for q in range(N) if q not in [d, mate] + xn]
+    order = late + xn + [mate, d] if SIDE[d] == 0 else [d, mate] + xn + late
+    first = 8 if SIDE[d] == 0 else ZA + CI
+    land = {q: first + CI * i for i, q in enumerate(order)}
+    if SIDE[d] == 0:
+        return land, (land[xn[0]], 3 * CI), (first, 5 * CI), 0
+    return land, (land[xn[0]] + CI - 128, 128), (first + SA - 128, 128), 128 - 5 * CI
 
 
 def plan(topo, q):
     me = CORES[q]
-    mate = [d for d in range(N) if topo.mates(topo.chip(me), topo.chip(CORES[d]))][0]
-    near = lambda d: GCOL[d] // 2 == GCOL[q] // 2
-    same = [d for d in range(N) if d != q and topo.same_plane(topo.chip(me), topo.chip(CORES[d]))]
-    cross = [d for d in range(N) if d != q and d != mate and d not in same]
-    sn, sf = [d for d in same if near(d)], [d for d in same if not near(d)]
-    xn, xf = [d for d in cross if near(d)], [d for d in cross if not near(d)]
+    mate, sn, sf, xn, xf = groups(topo, q)
     others = [c for c in topo.cores_of(me) if c != me]
-    ported = [c for c in others if topo.may_write(c, CORES[mate])]
-    plain = [c for c in others if c not in ported]
-    here = lambda c: topo.die(c) == topo.die(me)
-    c_xn = [c for c in ported if here(c)][0]
-    c_xfc, c_xfs = [c for c in ported if not here(c)][:2]
-    c_sfc, c_sfs = [c for c in plain if here(c)][:2]
-    c_snc, c_sns = [c for c in plain if not here(c)][:2]
-    hops = {"far": [c_xfc, c_sfc], "scales": [c_xfs, c_sfs, c_sns], "near": [c_xn, c_snc]}
-    sends = [(me, "codes", [mate], "tile"), (me, "scales", [mate] + xn, "tile"),
-             (c_xn, "codes", xn, "near"), (c_snc, "codes", sn, "near"),
-             (c_xfc, "codes", xf, "far"), (c_sfc, "codes", sf, "far"),
-             (c_xfs, "scales", xf, "scales"), (c_sfs, "scales", sf, "scales"), (c_sns, "scales", sn, "scales")]
-    return hops, sends
+    here = lambda cs: sorted(cs, key=lambda c: topo.die(c) != topo.die(me))
+    x1, x2, x3 = here([c for c in others if topo.may_write(c, CORES[mate])])[:3]
+    p = here([c for c in others if not topo.may_write(c, CORES[mate])])
+    s2, s1, s3 = p[0], p[2], p[1]
+    run = a_run(q)[1]
+    hops = {"hfc": [(x2, bsrc(q, xf[0])[2]), (s2, bsrc(q, sf[0])[2])], "hfs": [(x3, bsrc(q, xf[0])[2]), (s3, bsrc(q, sf[0])[2])],
+            "hnc": [(x1, bsrc(q, xn[0])[2]), (s1, bsrc(q, sn[0])[2])], "hns": [(x3, bsrc(q, xn[0])[2]), (s3, bsrc(q, sn[0])[2])],
+            "hac": [(x1, run), (s1, run)], "has": [(x2, run), (s2, run)]}
+    b = bsrc(q, mate)
+    sends = {me: [(None, "bc", [mate], b[0], b[2]), (None, "bs", [mate], b[1], b[2]),
+                  (None, "ac", [mate] + xn, "lac", run), (None, "as", [mate] + xn, "las", run)],
+             x1: [("hnc", "bc", xn, "hnc", 0), ("hac", "ac", xf, "hac", 0)],
+             s1: [("hnc", "bc", sn, "hnc", 0), ("hac", "ac", sf, "hac", 0), (None, "ac", sn, "hac", 0)],
+             x2: [("hfc", "bc", xf, "hfc", 0), ("has", "as", xf, "has", 0)],
+             s2: [("hfc", "bc", sf, "hfc", 0), ("has", "as", sf, "has", 0), (None, "as", sn, "has", 0)],
+             x3: [("hfs", "bs", xf, "hfs", 0), ("hns", "bs", xn, "hns", 0)],
+             s3: [("hfs", "bs", sf, "hfs", 0), ("hns", "bs", sn, "hns", 0)]}
+    return sends, hops
 
 
-def engine_parts(topo, src, dsts):
-    e = topo.engines(src, CORES[dsts[0]])
-    k = len(e) // len(dsts)
-    return [sum(1 << x for x in e[i * k:(i + 1) * k]) for i in range(len(dsts))]
+def masks(topo, src, dsts):
+    e = topo.engines(src, dsts[0])
+    return [sum(1 << x for x in e[i::len(dsts)]) for i in range(len(dsts))]
 
 
-def dst_id(topo, c):
-    rid, pid, _ = topo.addr(c)
-    return DstId(rid=rid, pnc=pid)
+def engines_in(m):
+    return bin(m).count("1")
 
 
-def hop(g, T, topo, core, src, dst, helpers, sem):
-    g.remote_dma_fused([RemoteDMATransfer(dst_ids=[dst_id(topo, c) for c in helpers],
-                                          dma_engine_mask=topo.mask(core, helpers[0]), remote_sem=T.sem[sem],
-                                          srcs=[src], dsts=[dst for _ in helpers], alu_op=0)], local_sem=T.sem.sent)
-    return len(topo.engines(core, helpers[0]))
+def arrival_sem(topo, d, q, kind):
+    mate, _, _, xn, _ = groups(topo, d)
+    return "arr%d" % away(d, q) if kind[0] == "b" else "arre" if q in [mate] + xn else "arrl"
 
 
-def send(g, T, topo, core, q, kind, dsts, source):
-    _, _, farb, nearb = layout(q)
-    buf, base = {"tile": ("qc" if kind == "codes" else "qs", 0), "far": ("hfc", farb), "near": ("hnc", nearb),
-                 "scales": ("hs", 0)}[source]
-    used = 0
-    for tile in ("b", "a"):
-        tr = []
-        for d, m in zip(dsts, engine_parts(topo, core, dsts)):
-            if tile == "b":
-                view, pos = bland(d, q)
-                s, e, w, land = bcol(q, d) - base, view + CJ * pos, CJ, "lb"
-            else:
-                s, e, w, land = acol(d) - base, aland(d, q), CI, "la"
-            if kind == "codes":
-                src, dst = T[buf][:, s:s + w].bitcast(dt.uint8), T[land + "c"][:, e:e + w].bitcast(dt.uint8)
-            else:
-                src, dst = T[buf][:, s:s + w], T[land + "s"][:, e:e + w]
-            tr.append(RemoteDMATransfer(dst_ids=[dst_id(topo, CORES[d])], dma_engine_mask=m, remote_sem=T.sem.arr,
-                                        srcs=[src], dsts=[dst], alu_op=0))
-            used += bin(m).count("1")
-        g.remote_dma_fused(tr, local_sem=T.sem.sent)
-    return used
+def view(T, name, c, w):
+    return T[name][:, c:c + w].bitcast(dt.uint8) if name[-1] == "c" else T[name][:, c:c + w]
+
+
+def fused(g, T, topo, core, parts):
+    ms = masks(topo, core, [x[0] for x in parts])
+    tr = []
+    for (c, sem, w, s, sc, d, dc), m in zip(parts, ms):
+        rid, pid, _ = topo.addr(c)
+        tr.append(RemoteDMATransfer(dst_ids=[DstId(rid=rid, pnc=pid)], dma_engine_mask=m, remote_sem=T.sem[sem],
+                                    srcs=[view(T, s, sc, w)], dsts=[view(T, d, dc, w)], alu_op=0))
+    g.remote_dma_fused(tr, local_sem=T.sem.sent)
+    return sum(engines_in(m) for m in ms)
+
+
+def send(g, T, topo, core, q, call):
+    _, kind, dsts, src, c0 = call
+    parts = []
+    for d in dsts:
+        if kind[0] == "b":
+            v0, pos = bland(d, q)
+            w, c, e = CJ, c0, v0 + CJ * pos
+        else:
+            w, c, e = CI, c0 + CI * SIDE[d], aland(topo, d)[0][q]
+        parts.append((CORES[d], arrival_sem(topo, d, q, kind), w, src, c, "l" + kind, e))
+    return fused(g, T, topo, core, parts)
+
+
+def hop(g, T, topo, core, buf, src, to):
+    w = 2 * CI if buf[1] == "a" else CJ
+    return fused(g, T, topo, core, [(c, buf, w, src, col, buf, 0) for c, col in to])
 
 
 def arrivals(topo, r):
-    n = 0
+    n = {}
     for q in range(N):
-        if q != r:
-            for c, _, dsts, _ in plan(topo, q)[1]:
-                for d, m in zip(dsts, engine_parts(topo, c, dsts)):
-                    n += 2 * bin(m).count("1") if d == r else 0
+        for c, calls in plan(topo, q)[0].items():
+            for _, kind, dsts, _, _ in calls:
+                for d, m in zip(dsts, masks(topo, c, [CORES[x] for x in dsts])):
+                    if d == r:
+                        s = arrival_sem(topo, r, q, kind)
+                        n[s] = n.get(s, 0) + engines_in(m)
     return n
 
 
 def helper_program(g, core, T, topo, q):
-    hops, sends = plan(topo, q)
-    sem = {"far": "hopf", "near": "hopn", "scales": "hops"}
+    sends, hops = plan(topo, q)
     used = 0
-    for c, kind, dsts, source in sends:
-        if c == core:
-            g.wait_ge(T.sem[sem[source]], len(topo.engines(CORES[q], core)))
-            used += send(g, T, topo, core, q, kind, dsts, source)
+    for call in sends.get(core, []):
+        if call[0]:
+            ms = masks(topo, CORES[q], [c for c, _ in hops[call[0]]])
+            g.wait_ge(T.sem[call[0]], [engines_in(m) for (c, _), m in zip(hops[call[0]], ms) if c == core][0])
+        used += send(g, T, topo, core, q, call)
     if used:
         g.wait_ge(T.sem.sent, used)
 
@@ -185,18 +216,18 @@ def rank_program(g, core, T, topo):
             helper_program(g, core, T, topo, q[0])
         return
     v, sc, sy, te, sem = g.vector, g.scalar, g.sync, g.tensor, T.sem
-    COPY = ActivationFunctionType.Copy
-    hops, sends = plan(topo, rank)
-    near, far, farb, nearb = layout(rank)
+    COPY, A = ActivationFunctionType.Copy, AluOpType
+    sends, hops = plan(topo, rank)
+    land, view1, view2, both = aland(topo, rank)
     kn = 8 * (GCOL[rank] // 2)
     kf = 8 - kn
-    oa = acol(rank)
 
     sy.dma_start(T.wb[:], T.b[:]).then_inc(sem.ldb, 16)
     for k in range(8):
-        sy.dma_start(T.lst[16 * k:16 * k + 16, 0:KB], T.sb[:]).then_inc(sem.lists, 16)
-        sc.dma_start(T.lst[16 * k:16 * k + 16, KB:LST], T.sa[:]).then_inc(sem.lists, 16)
-    sc.dma_start(T.wa[:], T.a[:]).then_inc(sem.lda, 16)
+        (sy if k < 4 else sc).dma_start(T.lsb[16 * k:16 * k + 16, :], T.sb[:]).then_inc(sem.listb, 16)
+    sy.dma_start(T.wa[:], T.a[:]).then_inc(sem.lda, 16)
+    for k in range(8):
+        (sy if k < 4 else sc).dma_start(T.lsa[16 * k:16 * k + 16, :], T.sa[:]).then_inc(sem.lista, 16)
     for k in range(8):
         sy.dma_start(T.pil[16 * k:16 * k + 16, :], T.pi[:]).then_inc(sem.ldpi, 16)
 
@@ -206,34 +237,32 @@ def rank_program(g, core, T, topo):
     g.indirect_dma_start(out=T.pjl[:, 0:24], out_offset=None, in_=T.pj[:],
                          in_offset=IndirectOffsetOnAxis(ap=T.part16[:, 0:1], axis=0),
                          bounds_check=15).then_inc(sem.ldpj, 16)
-    g.wait_ge(sem.onesd, 1)
-    g.affine_select(T.eye[:], T.ones[:], [[-1, 128]], AluOpType.is_equal, 0.0, 0, 1).then_inc(sem.eyed, 1)
-
     used = 0
-    g.wait_ge(sem.qfar, 1)
-    used += hop(g, T, topo, core, T.qc[:, farb:farb + FARW].bitcast(dt.uint8), T.hfc[:, 0:FARW].bitcast(dt.uint8),
-                hops["far"], "hopf")
-    g.wait_ge(sem.qnear, 1)
-    used += hop(g, T, topo, core, T.qs[:, 0:W], T.hs[:, 0:W], hops["scales"], "hops")
-    used += hop(g, T, topo, core, T.qc[:, nearb:nearb + NEARW].bitcast(dt.uint8), T.hnc[:, 0:NEARW].bitcast(dt.uint8),
-                hops["near"], "hopn")
-    for c, kind, dsts, source in sends:
-        if c == core:
-            used += send(g, T, topo, core, rank, kind, dsts, source)
+    for ready, codes, scales, src in (("qf", "hfc", "hfs", "q"), ("qn", "hnc", "hns", "lb"), ("qa", "hac", "has", "la")):
+        g.wait_ge(sem[ready], 1)
+        used += hop(g, T, topo, core, codes, src + "c", hops[codes])
+        used += hop(g, T, topo, core, scales, src + "s", hops[scales])
+    for call in sends[core]:
+        used += send(g, T, topo, core, rank, call)
 
-    v.memset(T.ones[:], 1.0).then_inc(sem.onesd, 1)
-    v.memset(T.inv[:], 999.0).then_inc(sem.filled, 1)
+    run, ablk = a_run(rank)
+    za = 2 * CI if ablk == run else 0
+    v.memset(T.ta[:, 4 * za:4 * (za + ZA)], 0.0).then_inc(sem.zeros, 1)
     v.wait_ge(sem.iota, 1)
-    v.tensor_scalar(T.part16[:], T.part[:], 15, None, AluOpType.bitwise_and).then_inc(sem.p16, 1)
+    v.tensor_scalar(T.part16[:], T.part[:], 15, None, A.bitwise_and).then_inc(sem.p16, 1)
+    v.tensor_copy(T.partf[:], T.part[:]).then_inc(sem.pf, 1)
+    v.memset(T.inv[:], 999.0).then_inc(sem.filled, 1)
 
-    def offsets(t, s):
-        v.tensor_scalar(T.off[:, UW * t:UW * t + LST], T.lst[:], 4, t, AluOpType.mult, AluOpType.add).then_inc(sem[s], 1)
+    def offsets(what, t, s):
+        out, lst, k, step = (T.offb, T.lsb, KB, KB) if what == "b" else (T.offa, T.lsa, KA, 4)
+        v.tensor_scalar(out[:, step * t:step * t + k], lst[:], 4, t, A.mult, A.add).then_inc(sem[s], 1)
 
     def blocks(t, what):
         if what == "a":
-            return T.h[:, 4 * APOS + t:4 * (APOS + 2 * CI):4], T.wa[:].indirect(T.off[:, UW * t + KB:UW * t + LST])
-        k, p = (kn, near) if what == "near" else (kf, far)
-        return T.h[:, 4 * p + t:4 * (p + PAIR):4], T.wb[:].indirect(T.off[:, UW * t + k:UW * t + k + 8])
+            c = 4 * (ablk - run)
+            return T.ta[:, c + t:c + 8 * CI:4], T.wa[:].indirect(T.offa[:, 4 * t:4 * t + KA])
+        k = KB * t + (kn if what == "near" else kf)
+        return (T.tn if what == "near" else T.tf)[:, t:4 * PAIR:4], T.wb[:].indirect(T.offb[:, k:k + 8])
 
     def gather_v(t, what, s):
         o, i = blocks(t, what)
@@ -243,42 +272,46 @@ def rank_program(g, core, T, topo):
         o, i = blocks(t, what)
         sc.activation(o, i, COPY).then_inc(sem[s], 1)
 
-    v.wait_ge(sem.lists, 256)
-    for t in (2, 3):
-        offsets(t, "offs")
-    for t in (0, 1):
-        offsets(t, "offv")
-    sc.wait_ge(sem.offs, 2)
+    v.wait_ge(sem.listb, 128)
+    offsets("b", 2, "off2")
+    offsets("b", 3, "off3")
+    offsets("b", 0, "offv")
+    offsets("b", 1, "offv")
     sc.wait_ge(sem.ldb, 16)
-    v.wait_ge(sem.offv, 2)
-    v.wait_ge(sem.ldb, 16)
+    sc.wait_ge(sem.off2, 1)
     gather_s(2, "far", "fars")
+    sc.wait_ge(sem.off3, 1)
     gather_s(3, "far", "fars")
     sc.wait_ge(sem.offv, 2)
-    sc.wait_ge(sem.lda, 16)
     for t in (1, 2, 3):
-        gather_s(t, "a", "fars")
+        gather_s(t, "near", "nears")
+    v.wait_ge(sem.offv, 2)
+    v.wait_ge(sem.ldb, 16)
     gather_v(0, "far", "farv")
     gather_v(1, "far", "farv")
-    v.wait_ge(sem.lda, 16)
-    gather_v(0, "a", "farv")
-    gather_s(2, "near", "nears")
-    gather_s(3, "near", "nears")
-    v.wait_ge(sem.farv, 3)
-    v.wait_ge(sem.fars, 5)
-    v.quantize_mx(T.qc[:, farb:farb + FARW], T.qs[:, farb:farb + FARW],
-                  T.h[:, 4 * farb:4 * (farb + FARW)]).then_inc(sem.qfar, 1)
+    v.wait_ge(sem.farv, 2)
+    v.wait_ge(sem.fars, 2)
+    v.quantize_mx(T.qc[:], T.qs[:], T.tf[:]).then_inc(sem.qf, 1)
     gather_v(0, "near", "nearv")
-    gather_v(1, "near", "nearv")
-    v.wait_ge(sem.nearv, 2)
-    v.wait_ge(sem.nears, 2)
-    v.quantize_mx(T.qc[:, near:near + PAIR], T.qs[:, near:near + PAIR],
-                  T.h[:, 4 * near:4 * (near + PAIR)]).then_inc(sem.qnear, 1)
-    view, pos = bland(rank, rank)
-    e = view + CJ * pos - CJ * (GCOL[rank] % 2)
-    v.quantize_mx(T.lbc[:, e:e + PAIR], T.lbs[:, e:e + PAIR], T.h[:, 4 * near:4 * (near + PAIR)]).then_inc(sem.qown, 1)
-    e = aland(rank, rank)
-    v.quantize_mx(T.lac[:, e:e + 128], T.las[:, e:e + 128], T.h[:, 4 * oa:4 * (oa + 128)]).then_inc(sem.qown, 1)
+    v.wait_ge(sem.lista, 128)
+    for t in (2, 3, 0, 1):
+        offsets("a", t, "offa")
+    v.wait_ge(sem.nearv, 1)
+    v.wait_ge(sem.nears, 3)
+    e = near_at(rank)
+    v.quantize_mx(T.lbc[:, e:e + PAIR], T.lbs[:, e:e + PAIR], T.tn[:]).then_inc(sem.qn, 1)
+    sc.wait_ge(sem.offa, 4)
+    sc.wait_ge(sem.lda, 16)
+    v.wait_ge(sem.offa, 4)
+    v.wait_ge(sem.lda, 16)
+    gather_s(2, "a", "as")
+    gather_s(3, "a", "as")
+    gather_v(0, "a", "av")
+    gather_v(1, "a", "av")
+    v.wait_ge(sem.zeros, 1)
+    v.wait_ge(sem.av, 2)
+    v.wait_ge(sem["as"], 2)
+    v.quantize_mx(T.lac[:, run:run + 128], T.las[:, run:run + 128], T.ta[:]).then_inc(sem.qa, 1)
 
     n = [0]
 
@@ -288,61 +321,81 @@ def rank_program(g, core, T, topo):
 
     def settle():
         v.wait_ge(sem.vc, n[0])
-    pos0 = bland(rank, 0)[1]
-    ca = aland(rank, 0) - LA0
-    A = AluOpType
-    v.wait_ge(sem.ldpi, 128)
-    done(v.tensor_scalar(T.pit[:], T.pil[:], ca, None, A.add))
+    shift = [land[q] - CI * q for q in range(N)]
+    jumps = [q for q in range(1, N) if shift[q] != shift[q - 1]]
     v.wait_ge(sem.ldpj, 16)
-    done(v.tensor_scalar(T.pjt[:], T.pjl[:], CJ * pos0, None, A.add))
+    done(v.tensor_scalar(T.pjt[:], T.pjl[:], CJ * bland(rank, 0)[1], None, A.add))
+    v.wait_ge(sem.ldpi, 128)
+    done(v.tensor_scalar(T.pit[:], T.pil[:], shift[0], None, A.add))
+    for q in jumps:
+        done(v.tensor_scalar(T.pim[:, 8 * q:8 * q + 8], T.pil[:], CI * q, shift[q] - shift[q - 1], A.is_ge, A.mult))
     settle()
-    done(v.tensor_scalar(T.pim[:], T.pit[:], SA, -SA, A.is_ge, A.mult))
     done(v.tensor_scalar(T.pju[:], T.pjt[:], SB - 1, None, A.bitwise_and))
-    settle()
-    done(v.tensor_tensor(T.pit[:], T.pit[:], T.pim[:], A.add))
+    for q in jumps:
+        done(v.tensor_tensor(T.pit[:], T.pit[:], T.pim[:, 8 * q:8 * q + 8], A.add))
+        settle()
+    done(v.tensor_copy(T.pio[:], T.pit[:]))
     done(v.tensor_copy(T.pjo[:], T.pju[:]))
     settle()
-    done(v.tensor_copy(T.pio[:], T.pit[:]))
-    settle()
+    sc.wait_ge(sem.vc, n[0])
     v.wait_ge(sem.filled, 1)
     v.wait_ge(sem.cnt, 1)
     done(v.tensor_copy(T.inv[:].indirect(T.pio[:, 0:8]), T.count[:]))
+    v.wait_ge(sem.pf, 1)
+    done(v.tensor_scalar(T.eye[:], T.count[:], T.partf[:, 0:1], None, A.is_equal))
     settle()
-    v.wait_ge(sem.eyed, 1)
-    done(v.tensor_tensor(T.dg1[:], T.inv[:, CJ:SA], T.eye[:], A.mult))
-    done(v.tensor_tensor(T.dg2[:], T.inv[:, 0:128], T.eye[:], A.mult))
+    for dg, (c, _) in (("dg1", view1), ("dg2", view2)):
+        done(v.tensor_tensor(T[dg][:], T.inv[:, c:c + 128], T.eye[:], A.mult))
     settle()
     done(v.tensor_reduce(T.ix1f[:], T.dg1[:], AxisListType.X, A.add))
     done(v.tensor_reduce(T.ix2f[:], T.dg2[:], AxisListType.X, A.add))
     settle()
+    if both:
+        done(v.memset(T.ix2f[0:both, :], 999.0))
+        settle()
     v.tensor_copy(T.ix1[:], T.ix1f[:]).then_inc(sem.ixd, 1)
     v.tensor_copy(T.ix2[:], T.ix2f[:]).then_inc(sem.ixd, 1)
-    sc.wait_ge(sem.vc, n[0])
 
-    te.wait_ge(sem.qown, 2)
-    te.wait_ge(sem.arr, arrivals(topo, rank))
-    hb = SB // 2
-    for i in range(4):
-        a0, b0 = LA0 + (SA - 128 if i < 2 else 0), view + hb * (i % 2)
-        te.matmul_mx(T.ps[:, 512 * i:512 * i + hb], T.lac[:, a0:a0 + 128], T.las[:, a0:a0 + 128],
-                     T.lbc[:, b0:b0 + hb], T.lbs[:, b0:b0 + hb], True, True).then_inc(sem["m%d" % i], 1)
+    counts = arrivals(topo, rank)
+    v0 = bland(rank, rank)[0]
+    lead = GCOL[rank] % 2 == 0
+    order = (0, 2, 1)
+    need = {0: ["arr1"] + (["arr0"] if lead else []), 2: ["arr3"] + ([] if lead else ["arr0"]), 1: ["arr2"]}
+    te.wait_ge(sem.qn, 1)
+    te.wait_ge(sem.qa, 1)
+    te.wait_ge(sem.arre, counts["arre"])
+    for i in range(6):
+        if i < 3:
+            for s in need[order[i]]:
+                te.wait_ge(sem[s], counts[s])
+        if i == 3:
+            te.wait_ge(sem.arrl, counts["arrl"])
+        a0 = (view1 if i < 3 else view2)[0]
+        b0, b1 = CHUNKS[order[i % 3]]
+        te.matmul_mx(T.ps[:, 512 * i:512 * i + b1 - b0], T.lac[:, a0:a0 + 128], T.las[:, a0:a0 + 128],
+                     T.lbc[:, v0 + b0:v0 + b1], T.lbs[:, v0 + b0:v0 + b1], True, True).then_inc(sem["m%d" % i], 1)
     for i in (1, 2):
         s, y, hy = T["s%d" % i], T["y%d" % i], JW // 2
         cv, cs, yd = sem["c%dv" % i], sem["c%ds" % i], sem["yd%d" % i]
-        p = 1024 * (i - 1)
-        v.wait_ge(sem["m%d" % (2 * i - 2)], 1)
-        v.tensor_copy(s[:, 0:hb], T.ps[:, p:p + hb]).then_inc(cv, 1)
-        sc.wait_ge(sem["m%d" % (2 * i - 1)], 1)
-        sc.activation(s[:, hb:SB], T.ps[:, p + 512:p + 512 + hb], COPY).then_inc(cs, 1)
-        v.wait_ge(cv, 1)
+        for k in range(3):
+            m = 3 * (i - 1) + k
+            b0, b1 = CHUNKS[order[k]]
+            src, dst = T.ps[:, 512 * m:512 * m + b1 - b0], s[:, b0:b1]
+            if k == 0:
+                sc.wait_ge(sem["m%d" % m], 1)
+                sc.activation(dst, src, COPY).then_inc(cs, 1)
+            else:
+                v.wait_ge(sem["m%d" % m], 1)
+                v.tensor_copy(dst, src).then_inc(cv, 1)
+        v.wait_ge(cv, 2)
         v.wait_ge(cs, 1)
         v.tensor_copy(y[:, 0:hy], s[:].indirect(T.pjo[:, 0:12])).then_inc(yd, 1)
-        sc.wait_ge(cv, 1)
+        sc.wait_ge(cv, 2)
         sc.wait_ge(cs, 1)
         sc.activation(y[:, hy:JW], s[:].indirect(T.pjo[:, 12:24]), COPY).then_inc(yd, 1)
 
     g.wait_ge(sem.ixd, 2)
-    for i, rows in ((1, 128), (2, SA - 128)):
+    for i, rows in ((1, view1[1]), (2, view2[1])):
         g.wait_ge(sem["yd%d" % i], 2)
         g.indirect_dma_start(out=T.y[:], out_offset=IndirectOffsetOnAxis(ap=T["ix%d" % i][0:rows, 0:1], axis=0),
                              in_=T["y%d" % i][0:rows, 0:JW], in_offset=None, bounds_check=M - 1,

from concourse.bass import DstId, RemoteDMATransfer, IndirectOffsetOnAxis
from concourse.mybir import dt, AluOpType, AxisListType, ActivationFunctionType

CORES = [3, 11, 19, 27, 35, 43, 51, 59]
N = 8
TA, TB, CI, CJ, JW, M = 256, 256, 24, 64, 384, 128
SIDE = [r // 4 for r in range(N)]
GCOL = [r % 4 for r in range(N)]
PAIR = 2 * CJ
SA, SB = N * CI, N * CJ
KB, KA = 16, 3
LAW = 304
ZA = 128 - 2 * CI
CHUNKS = ((0, 3 * CJ), (3 * CJ, 5 * CJ), (5 * CJ, 8 * CJ))

SCRATCH = {
    "wa": ("sbuf", [128, 4 * TA], "bfloat16"),
    "wb": ("sbuf", [128, 4 * TB], "bfloat16"),
    "lsb": ("sbuf", [128, KB], "int32"),
    "lsa": ("sbuf", [128, KA], "int32"),
    "offb": ("sbuf", [128, 4 * KB], "uint16"),
    "offa": ("sbuf", [128, 16], "uint16"),
    "tf": ("sbuf", [128, 4 * PAIR], "bfloat16"),
    "tn": ("sbuf", [128, 4 * PAIR], "bfloat16"),
    "ta": ("sbuf", [128, 4 * 128], "bfloat16"),
    "qc": ("sbuf", [128, PAIR], "float8_e4m3fn_x4"),
    "qs": ("sbuf", [128, PAIR], "uint8"),
    "hfc": ("sbuf", [128, CJ], "float8_e4m3fn_x4"),
    "hfs": ("sbuf", [128, CJ], "uint8"),
    "hnc": ("sbuf", [128, CJ], "float8_e4m3fn_x4"),
    "hns": ("sbuf", [128, CJ], "uint8"),
    "hac": ("sbuf", [128, 2 * CI], "float8_e4m3fn_x4"),
    "has": ("sbuf", [128, 2 * CI], "uint8"),
    "lac": ("sbuf", [128, LAW], "float8_e4m3fn_x4"),
    "las": ("sbuf", [128, LAW], "uint8"),
    "lbc": ("sbuf", [128, SB + CJ], "float8_e4m3fn_x4"),
    "lbs": ("sbuf", [128, SB + CJ], "uint8"),
    "pil": ("sbuf", [128, 8], "int32"),
    "pit": ("sbuf", [128, 8], "int32"),
    "pim": ("sbuf", [128, 8 * N], "int32"),
    "pio": ("sbuf", [128, 8], "uint16"),
    "pjl": ("sbuf", [128, 24], "int32"),
    "pjt": ("sbuf", [128, 24], "int32"),
    "pju": ("sbuf", [128, 24], "int32"),
    "pjo": ("sbuf", [128, 24], "uint16"),
    "part": ("sbuf", [128, 1], "int32"),
    "part16": ("sbuf", [128, 1], "int32"),
    "partf": ("sbuf", [128, 1], "float32"),
    "count": ("sbuf", [128, 128], "float32"),
    "eye": ("sbuf", [128, 128], "float32"),
    "inv": ("sbuf", [128, LAW], "float32"),
    "dg1": ("sbuf", [128, 128], "float32"),
    "dg2": ("sbuf", [128, 128], "float32"),
    "ix1f": ("sbuf", [128, 1], "float32"),
    "ix2f": ("sbuf", [128, 1], "float32"),
    "ix1": ("sbuf", [128, 1], "int32"),
    "ix2": ("sbuf", [128, 1], "int32"),
    "s1": ("sbuf", [128, SB], "float32"),
    "s2": ("sbuf", [128, SB], "float32"),
    "y1": ("sbuf", [128, JW], "float32"),
    "y2": ("sbuf", [128, JW], "float32"),
    "ps": ("psum", [128, 6 * 512], "float32"),
}
SEMAPHORES = ["listb", "lista", "ldb", "lda", "ldpi", "ldpj", "iota", "cnt", "filled", "zeros", "p16", "pf",
              "off2", "off3", "offv", "offa", "fars", "farv", "nears", "nearv", "as", "av", "qf", "qn", "qa", "vc", "ixd",
              "hfc", "hfs", "hnc", "hns", "hac", "has", "arre", "arrl", "arr0", "arr1", "arr2", "arr3", "sent",
              "m0", "m1", "m2", "m3", "m4", "m5", "c1v", "c1s", "c2v", "c2s", "yd1", "yd2", "ystored"]


def bland(d, q):
    if GCOL[d] % 2 == 0:
        return 0, (q - d - 1) % N
    return CJ, (q - d) % N


def near_at(r):
    view, pos = bland(r, r)
    return view + CJ * pos - CJ * (GCOL[r] % 2)


def bsrc(q, d):
    if GCOL[d] // 2 == GCOL[q] // 2:
        return "lbc", "lbs", near_at(q) + CJ * (GCOL[d] % 2)
    return "qc", "qs", CJ * (GCOL[d] % 2)


def a_run(r):
    return (176, 176) if SIDE[r] == 0 else (0, ZA)


def away(d, q):
    return (q // 2 - d // 2) % 4


def groups(topo, q):
    chip = [topo.chip(c) for c in CORES]
    mate = [d for d in range(N) if topo.mates(chip[q], chip[d])][0]
    same = [d for d in range(N) if d != q and topo.same_plane(chip[q], chip[d])]
    cross = [d for d in range(N) if d not in same + [q, mate]]
    near = lambda ds: [d for d in ds if GCOL[d] // 2 == GCOL[q] // 2]
    far = lambda ds: [d for d in ds if GCOL[d] // 2 != GCOL[q] // 2]
    return mate, near(same), far(same), near(cross), far(cross)


def aland(topo, d):
    mate, _, _, xn, _ = groups(topo, d)
    late = [q for q in range(N) if q not in [d, mate] + xn]
    order = late + xn + [mate, d] if SIDE[d] == 0 else [d, mate] + xn + late
    first = 8 if SIDE[d] == 0 else ZA + CI
    land = {q: first + CI * i for i, q in enumerate(order)}
    if SIDE[d] == 0:
        return land, (land[xn[0]], 3 * CI), (first, 5 * CI), 0
    return land, (land[xn[0]] + CI - 128, 128), (first + SA - 128, 128), 128 - 5 * CI


def plan(topo, q):
    me = CORES[q]
    mate, sn, sf, xn, xf = groups(topo, q)
    others = [c for c in topo.cores_of(me) if c != me]
    here = lambda cs: sorted(cs, key=lambda c: topo.die(c) != topo.die(me))
    x1, x2, x3 = here([c for c in others if topo.may_write(c, CORES[mate])])[:3]
    p = here([c for c in others if not topo.may_write(c, CORES[mate])])
    s2, s1, s3 = p[0], p[2], p[1]
    run = a_run(q)[1]
    hops = {"hfc": [(x2, bsrc(q, xf[0])[2]), (s2, bsrc(q, sf[0])[2])], "hfs": [(x3, bsrc(q, xf[0])[2]), (s3, bsrc(q, sf[0])[2])],
            "hnc": [(x1, bsrc(q, xn[0])[2]), (s1, bsrc(q, sn[0])[2])], "hns": [(x3, bsrc(q, xn[0])[2]), (s3, bsrc(q, sn[0])[2])],
            "hac": [(x1, run), (s1, run)], "has": [(x2, run), (s2, run)]}
    b = bsrc(q, mate)
    sends = {me: [(None, "bc", [mate], b[0], b[2]), (None, "bs", [mate], b[1], b[2]),
                  (None, "ac", [mate] + xn, "lac", run), (None, "as", [mate] + xn, "las", run)],
             x1: [("hnc", "bc", xn, "hnc", 0), ("hac", "ac", xf, "hac", 0)],
             s1: [("hnc", "bc", sn, "hnc", 0), ("hac", "ac", sf, "hac", 0), (None, "ac", sn, "hac", 0)],
             x2: [("hfc", "bc", xf, "hfc", 0), ("has", "as", xf, "has", 0)],
             s2: [("hfc", "bc", sf, "hfc", 0), ("has", "as", sf, "has", 0), (None, "as", sn, "has", 0)],
             x3: [("hfs", "bs", xf, "hfs", 0), ("hns", "bs", xn, "hns", 0)],
             s3: [("hfs", "bs", sf, "hfs", 0), ("hns", "bs", sn, "hns", 0)]}
    return sends, hops


def masks(topo, src, dsts):
    e = topo.engines(src, dsts[0])
    return [sum(1 << x for x in e[i::len(dsts)]) for i in range(len(dsts))]


def engines_in(m):
    return bin(m).count("1")


def arrival_sem(topo, d, q, kind):
    mate, _, _, xn, _ = groups(topo, d)
    return "arr%d" % away(d, q) if kind[0] == "b" else "arre" if q in [mate] + xn else "arrl"


def view(T, name, c, w):
    return T[name][:, c:c + w].bitcast(dt.uint8) if name[-1] == "c" else T[name][:, c:c + w]


def fused(g, T, topo, core, parts):
    ms = masks(topo, core, [x[0] for x in parts])
    tr = []
    for (c, sem, w, s, sc, d, dc), m in zip(parts, ms):
        rid, pid, _ = topo.addr(c)
        tr.append(RemoteDMATransfer(dst_ids=[DstId(rid=rid, pnc=pid)], dma_engine_mask=m, remote_sem=T.sem[sem],
                                    srcs=[view(T, s, sc, w)], dsts=[view(T, d, dc, w)], alu_op=0))
    g.remote_dma_fused(tr, local_sem=T.sem.sent)
    return sum(engines_in(m) for m in ms)


def send(g, T, topo, core, q, call):
    _, kind, dsts, src, c0 = call
    parts = []
    for d in dsts:
        if kind[0] == "b":
            v0, pos = bland(d, q)
            w, c, e = CJ, c0, v0 + CJ * pos
        else:
            w, c, e = CI, c0 + CI * SIDE[d], aland(topo, d)[0][q]
        parts.append((CORES[d], arrival_sem(topo, d, q, kind), w, src, c, "l" + kind, e))
    return fused(g, T, topo, core, parts)


def hop(g, T, topo, core, buf, src, to):
    w = 2 * CI if buf[1] == "a" else CJ
    return fused(g, T, topo, core, [(c, buf, w, src, col, buf, 0) for c, col in to])


def arrivals(topo, r):
    n = {}
    for q in range(N):
        for c, calls in plan(topo, q)[0].items():
            for _, kind, dsts, _, _ in calls:
                for d, m in zip(dsts, masks(topo, c, [CORES[x] for x in dsts])):
                    if d == r:
                        s = arrival_sem(topo, r, q, kind)
                        n[s] = n.get(s, 0) + engines_in(m)
    return n


def helper_program(g, core, T, topo, q):
    sends, hops = plan(topo, q)
    used = 0
    for call in sends.get(core, []):
        if call[0]:
            ms = masks(topo, CORES[q], [c for c, _ in hops[call[0]]])
            g.wait_ge(T.sem[call[0]], [engines_in(m) for (c, _), m in zip(hops[call[0]], ms) if c == core][0])
        used += send(g, T, topo, core, q, call)
    if used:
        g.wait_ge(T.sem.sent, used)


def rank_program(g, core, T, topo):
    rank = T.rank_of(core)
    if rank is None:
        q = [r for r in range(N) if topo.chip(CORES[r]) == topo.chip(core)]
        if q:
            helper_program(g, core, T, topo, q[0])
        return
    v, sc, sy, te, sem = g.vector, g.scalar, g.sync, g.tensor, T.sem
    COPY, A = ActivationFunctionType.Copy, AluOpType
    sends, hops = plan(topo, rank)
    land, view1, view2, both = aland(topo, rank)
    kn = 8 * (GCOL[rank] // 2)
    kf = 8 - kn

    sy.dma_start(T.wb[:], T.b[:]).then_inc(sem.ldb, 16)
    for k in range(8):
        (sy if k < 4 else sc).dma_start(T.lsb[16 * k:16 * k + 16, :], T.sb[:]).then_inc(sem.listb, 16)
    sy.dma_start(T.wa[:], T.a[:]).then_inc(sem.lda, 16)
    for k in range(8):
        (sy if k < 4 else sc).dma_start(T.lsa[16 * k:16 * k + 16, :], T.sa[:]).then_inc(sem.lista, 16)
    for k in range(8):
        sy.dma_start(T.pil[16 * k:16 * k + 16, :], T.pi[:]).then_inc(sem.ldpi, 16)

    g.iota(T.part[:], [[1, 1]], 0, 1).then_inc(sem.iota, 1)
    g.iota(T.count[:], [[1, 128]], 0, 0, allow_small_or_imprecise_dtypes=True).then_inc(sem.cnt, 1)
    g.wait_ge(sem.p16, 1)
    g.indirect_dma_start(out=T.pjl[:, 0:24], out_offset=None, in_=T.pj[:],
                         in_offset=IndirectOffsetOnAxis(ap=T.part16[:, 0:1], axis=0),
                         bounds_check=15).then_inc(sem.ldpj, 16)
    used = 0
    for ready, codes, scales, src in (("qf", "hfc", "hfs", "q"), ("qn", "hnc", "hns", "lb"), ("qa", "hac", "has", "la")):
        g.wait_ge(sem[ready], 1)
        used += hop(g, T, topo, core, codes, src + "c", hops[codes])
        used += hop(g, T, topo, core, scales, src + "s", hops[scales])
    for call in sends[core]:
        used += send(g, T, topo, core, rank, call)

    run, ablk = a_run(rank)
    za = 2 * CI if ablk == run else 0
    v.memset(T.ta[:, 4 * za:4 * (za + ZA)], 0.0).then_inc(sem.zeros, 1)
    v.wait_ge(sem.iota, 1)
    v.tensor_scalar(T.part16[:], T.part[:], 15, None, A.bitwise_and).then_inc(sem.p16, 1)
    v.tensor_copy(T.partf[:], T.part[:]).then_inc(sem.pf, 1)
    v.memset(T.inv[:], 999.0).then_inc(sem.filled, 1)

    def offsets(what, t, s):
        out, lst, k, step = (T.offb, T.lsb, KB, KB) if what == "b" else (T.offa, T.lsa, KA, 4)
        v.tensor_scalar(out[:, step * t:step * t + k], lst[:], 4, t, A.mult, A.add).then_inc(sem[s], 1)

    def blocks(t, what):
        if what == "a":
            c = 4 * (ablk - run)
            return T.ta[:, c + t:c + 8 * CI:4], T.wa[:].indirect(T.offa[:, 4 * t:4 * t + KA])
        k = KB * t + (kn if what == "near" else kf)
        return (T.tn if what == "near" else T.tf)[:, t:4 * PAIR:4], T.wb[:].indirect(T.offb[:, k:k + 8])

    def gather_v(t, what, s):
        o, i = blocks(t, what)
        v.tensor_copy(o, i).then_inc(sem[s], 1)

    def gather_s(t, what, s):
        o, i = blocks(t, what)
        sc.activation(o, i, COPY).then_inc(sem[s], 1)

    v.wait_ge(sem.listb, 128)
    offsets("b", 2, "off2")
    offsets("b", 3, "off3")
    offsets("b", 0, "offv")
    offsets("b", 1, "offv")
    sc.wait_ge(sem.ldb, 16)
    sc.wait_ge(sem.off2, 1)
    gather_s(2, "far", "fars")
    sc.wait_ge(sem.off3, 1)
    gather_s(3, "far", "fars")
    sc.wait_ge(sem.offv, 2)
    for t in (1, 2, 3):
        gather_s(t, "near", "nears")
    v.wait_ge(sem.offv, 2)
    v.wait_ge(sem.ldb, 16)
    gather_v(0, "far", "farv")
    gather_v(1, "far", "farv")
    v.wait_ge(sem.farv, 2)
    v.wait_ge(sem.fars, 2)
    v.quantize_mx(T.qc[:], T.qs[:], T.tf[:]).then_inc(sem.qf, 1)
    gather_v(0, "near", "nearv")
    v.wait_ge(sem.lista, 128)
    for t in (2, 3, 0, 1):
        offsets("a", t, "offa")
    v.wait_ge(sem.nearv, 1)
    v.wait_ge(sem.nears, 3)
    e = near_at(rank)
    v.quantize_mx(T.lbc[:, e:e + PAIR], T.lbs[:, e:e + PAIR], T.tn[:]).then_inc(sem.qn, 1)
    sc.wait_ge(sem.offa, 4)
    sc.wait_ge(sem.lda, 16)
    v.wait_ge(sem.offa, 4)
    v.wait_ge(sem.lda, 16)
    gather_s(2, "a", "as")
    gather_s(3, "a", "as")
    gather_v(0, "a", "av")
    gather_v(1, "a", "av")
    v.wait_ge(sem.zeros, 1)
    v.wait_ge(sem.av, 2)
    v.wait_ge(sem["as"], 2)
    v.quantize_mx(T.lac[:, run:run + 128], T.las[:, run:run + 128], T.ta[:]).then_inc(sem.qa, 1)

    n = [0]

    def done(ins):
        ins.then_inc(sem.vc, 1)
        n[0] += 1

    def settle():
        v.wait_ge(sem.vc, n[0])
    shift = [land[q] - CI * q for q in range(N)]
    jumps = [q for q in range(1, N) if shift[q] != shift[q - 1]]
    v.wait_ge(sem.ldpj, 16)
    done(v.tensor_scalar(T.pjt[:], T.pjl[:], CJ * bland(rank, 0)[1], None, A.add))
    v.wait_ge(sem.ldpi, 128)
    done(v.tensor_scalar(T.pit[:], T.pil[:], shift[0], None, A.add))
    for q in jumps:
        done(v.tensor_scalar(T.pim[:, 8 * q:8 * q + 8], T.pil[:], CI * q, shift[q] - shift[q - 1], A.is_ge, A.mult))
    settle()
    done(v.tensor_scalar(T.pju[:], T.pjt[:], SB - 1, None, A.bitwise_and))
    for q in jumps:
        done(v.tensor_tensor(T.pit[:], T.pit[:], T.pim[:, 8 * q:8 * q + 8], A.add))
        settle()
    done(v.tensor_copy(T.pio[:], T.pit[:]))
    done(v.tensor_copy(T.pjo[:], T.pju[:]))
    settle()
    sc.wait_ge(sem.vc, n[0])
    v.wait_ge(sem.filled, 1)
    v.wait_ge(sem.cnt, 1)
    done(v.tensor_copy(T.inv[:].indirect(T.pio[:, 0:8]), T.count[:]))
    v.wait_ge(sem.pf, 1)
    done(v.tensor_scalar(T.eye[:], T.count[:], T.partf[:, 0:1], None, A.is_equal))
    settle()
    for dg, (c, _) in (("dg1", view1), ("dg2", view2)):
        done(v.tensor_tensor(T[dg][:], T.inv[:, c:c + 128], T.eye[:], A.mult))
    settle()
    done(v.tensor_reduce(T.ix1f[:], T.dg1[:], AxisListType.X, A.add))
    done(v.tensor_reduce(T.ix2f[:], T.dg2[:], AxisListType.X, A.add))
    settle()
    if both:
        done(v.memset(T.ix2f[0:both, :], 999.0))
        settle()
    v.tensor_copy(T.ix1[:], T.ix1f[:]).then_inc(sem.ixd, 1)
    v.tensor_copy(T.ix2[:], T.ix2f[:]).then_inc(sem.ixd, 1)

    counts = arrivals(topo, rank)
    v0 = bland(rank, rank)[0]
    lead = GCOL[rank] % 2 == 0
    order = (0, 2, 1)
    need = {0: ["arr1"] + (["arr0"] if lead else []), 2: ["arr3"] + ([] if lead else ["arr0"]), 1: ["arr2"]}
    te.wait_ge(sem.qn, 1)
    te.wait_ge(sem.qa, 1)
    te.wait_ge(sem.arre, counts["arre"])
    for i in range(6):
        if i < 3:
            for s in need[order[i]]:
                te.wait_ge(sem[s], counts[s])
        if i == 3:
            te.wait_ge(sem.arrl, counts["arrl"])
        a0 = (view1 if i < 3 else view2)[0]
        b0, b1 = CHUNKS[order[i % 3]]
        te.matmul_mx(T.ps[:, 512 * i:512 * i + b1 - b0], T.lac[:, a0:a0 + 128], T.las[:, a0:a0 + 128],
                     T.lbc[:, v0 + b0:v0 + b1], T.lbs[:, v0 + b0:v0 + b1], True, True).then_inc(sem["m%d" % i], 1)
    for i in (1, 2):
        s, y, hy = T["s%d" % i], T["y%d" % i], JW // 2
        cv, cs, yd = sem["c%dv" % i], sem["c%ds" % i], sem["yd%d" % i]
        for k in range(3):
            m = 3 * (i - 1) + k
            b0, b1 = CHUNKS[order[k]]
            src, dst = T.ps[:, 512 * m:512 * m + b1 - b0], s[:, b0:b1]
            if k == 0:
                sc.wait_ge(sem["m%d" % m], 1)
                sc.activation(dst, src, COPY).then_inc(cs, 1)
            else:
                v.wait_ge(sem["m%d" % m], 1)
                v.tensor_copy(dst, src).then_inc(cv, 1)
        v.wait_ge(cv, 2)
        v.wait_ge(cs, 1)
        v.tensor_copy(y[:, 0:hy], s[:].indirect(T.pjo[:, 0:12])).then_inc(yd, 1)
        sc.wait_ge(cv, 2)
        sc.wait_ge(cs, 1)
        sc.activation(y[:, hy:JW], s[:].indirect(T.pjo[:, 12:24]), COPY).then_inc(yd, 1)

    g.wait_ge(sem.ixd, 2)
    for i, rows in ((1, view1[1]), (2, view2[1])):
        g.wait_ge(sem["yd%d" % i], 2)
        g.indirect_dma_start(out=T.y[:], out_offset=IndirectOffsetOnAxis(ap=T["ix%d" % i][0:rows, 0:1], axis=0),
                             in_=T["y%d" % i][0:rows, 0:JW], in_offset=None, bounds_check=M - 1,
                             oob_is_err=False).then_inc(sem.ystored, 16)
    g.wait_ge(sem.sent, used)
    g.wait_ge(sem.ystored, 32)
